import numpy as np
import ml_dtypes


def mxq(x, axis, fmt="e4m3"):
    dtype, down = {"e4m3": (ml_dtypes.float8_e4m3fn, 7), "e5m2": (ml_dtypes.float8_e5m2, 14)}[fmt]
    v = np.moveaxis(np.asarray(x, np.float32).astype(ml_dtypes.bfloat16).astype(np.float64), axis, -1)
    blocks = v.reshape(v.shape[:-1] + (-1, 32))
    amax = np.abs(blocks).max(-1, keepdims=True)
    byte = np.maximum(np.where(amax > 0, np.frexp(amax)[1] - 1 + 127, 0) - down, 1)
    scale = np.exp2(byte - 127.0)
    codes = (blocks / scale).astype(np.float32).astype(dtype).astype(np.float64)
    return np.moveaxis((codes * scale).reshape(v.shape), -1, axis)


WIDE = False


def mx_kscale(k):
    if not WIDE:
        return np.ones(k)
    levels = np.array([10, -10, 5, -5, 0])
    if k % 512:
        return np.exp2(np.random.permutation(np.resize(levels, k // 32))).repeat(32)
    a = np.empty((k // 512, 16))
    for p in range(k // 512):
        a[p, :8] = np.random.permutation(np.resize(levels, 8))
        for g in range(8):
            far = levels[np.abs(levels - a[p, g]) >= 10]
            a[p, g + 8] = far[np.random.randint(len(far))]
    return np.exp2(a.ravel()).repeat(32)


def f64(x):
    return np.asarray(x).astype(np.float64)


def striped(idx):
    return np.tile(idx.reshape(-1, 16).T, (8, 1)).astype(np.uint16)


def unstriped(offs):
    return offs[:16].T.reshape(-1).astype(np.int64)


def striped8(idx):
    return np.concatenate([x.reshape(-1, 16).T for x in idx]).astype(np.uint16)


def runs(offs, k):
    lists = np.stack([offs[16 * r : 16 * r + 16].T.reshape(-1) for r in range(8)]).astype(np.int64)
    return lists[np.arange(k) % 512 // 64]


def pack_weight(w):
    k, n = w.shape
    w = f64(np.asarray(w, np.float32).astype(ml_dtypes.bfloat16)).reshape(k // 32, 32, n)
    amax = np.abs(w).max(1)
    byte = np.clip(np.where(amax > 0, np.frexp(amax)[1] - 1 + 127 - 7, 1), 1, 254)
    scaled = (w * np.exp2(127.0 - byte)[:, None, :]).reshape(k, n).astype(np.float32)
    words = np.ascontiguousarray(scaled.reshape(k // 512, 128, 4, n).transpose(0, 1, 3, 2)).astype(ml_dtypes.float8_e4m3fn).view(np.uint8)
    return words, np.ascontiguousarray(byte.astype(np.uint8).reshape(k // 512, 16, n))


def unpack_weight(words, scales):
    g, p, n, _ = words.shape
    vals = np.ascontiguousarray(words).view(ml_dtypes.float8_e4m3fn).astype(np.float64) * np.repeat(np.exp2(scales.astype(np.float64) - 127.0), 8, axis=1)[..., None]
    return vals.transpose(0, 1, 3, 2).reshape(g * 512, n)


K, T, S, H, C, U = 512, 2048, 256, 512, 512, 512


def setup_inputs():
    n = np.random.standard_normal
    s = mx_kscale(K)[:, None]
    packed_xT = pack_weight(n((K, T)) * s)
    perm = np.random.permutation(U)
    return {
        "x_words": packed_xT[0],
        "x_scales": packed_xT[1],
        "w1": (n((K, H)) / np.sqrt(K) / s).astype(np.float32),
        "gs": (np.random.uniform(0.5, 1.5, (K, 1)) / s).astype(np.float32),
        "offs": striped(np.random.permutation(T)[:S]),
        "n1": striped8(np.stack([np.random.permutation(S) for _ in range(8)])),
        "n2": striped8(np.stack([np.random.permutation(S) for _ in range(8)])),
        "n3": striped8(np.stack([np.random.permutation(S) for _ in range(8)])),
        "cand": striped(np.random.permutation(T)[:C]),
        "n4": striped(perm[:S]),
        "n5": striped(perm[S:]),
        "n6": striped(np.random.permutation(U)),
    }


def reference(x_words, x_scales, w1, gs, offs, n1, n2, n3, cand, n4, n5, n6):
    x_cand = unpack_weight(x_words, x_scales)[:, unstriped(cand)]
    xq = unpack_weight(x_words, x_scales)[:, unstriped(offs)]
    y = mxq(f64(w1), 0, "e4m3").T @ xq
    st = y[np.arange(H)[:, None], runs(n1, H)] - (y[np.arange(H)[:, None], runs(n2, H)])
    z = f64(gs) * (np.maximum(st, st[np.arange(H)[:, None], runs(n3, H)]))
    s = 0.0625 * ((x_cand.T @ mxq(z, 0, "e4m3")))
    nw = 0.5 * s
    ph = np.zeros((C, U))
    ph[:, unstriped(n4)] = s
    pg = ph.copy()
    pg[:, unstriped(n5)] = nw
    return pg - pg[:, unstriped(n6)]

@@ -1,0 +1,163 @@
+from contextlib import ExitStack
+
+import concourse.mybir as mybir
+
+F32 = mybir.dt.float32
+BF16 = mybir.dt.bfloat16
+I32 = mybir.dt.int32
+U32 = mybir.dt.uint32
+U16 = mybir.dt.uint16
+U8 = mybir.dt.uint8
+FP8X4 = mybir.dt.float8_e4m3fn_x4
+COPY = mybir.ActivationFunctionType.Copy
+ALU = mybir.AluOpType
+
+P = 128
+PACK = 4
+T = 2048
+S = 256
+H = 512
+C = 512
+U = 512
+LANES = 16
+BLOCKS = C // P
+FIRST = 64
+FLOPS = 2 * 512 * H * S + 2 * 512 * C * S
+
+
+def entries(tile, lo, hi):
+    return tile[:, lo // LANES : hi // LANES]
+
+
+def tile_picked_candgapmxpagtwo_none_p_kernel(tc, x_words, x_scales, w1, gs, offs, n1, n2, n3, cand, n4, n5, n6, out):
+    nc = tc.nc
+    with ExitStack() as ctx:
+        lists = ctx.enter_context(tc.tile_pool(name="lists", bufs=1))
+        sb = ctx.enter_context(tc.tile_pool(name="sb", bufs=1))
+        psum = ctx.enter_context(tc.psum_pool(name="psum", bufs=1))
+
+        def load_list(src, name):
+            tile = lists.tile(list(src.shape), U16, name=name)
+            nc.sync.dma_start(tile[:], src)
+            return tile
+
+        xs = sb.tile([P, T], U8, name="xs", align_bytes=64)
+        nc.vector.memset(xs[:].bitcast(I32), 0)
+        w_raw = sb.tile([P, PACK, H], F32, name="w_raw")
+        nc.sync.dma_start(w_raw[:], w1.rearrange("(p j) c -> p j c", j=PACK))
+        for q in range(4):
+            nc.sync.dma_start(xs[32 * q : 32 * q + 4, :].bitcast(I32), x_scales[0, 4 * q : 4 * q + 4, :].bitcast(I32))
+        offs_t = load_list(offs, "offs_t")
+        xw = sb.tile([P, T], U32, name="xw", align_bytes=64)
+        nc.sync.dma_start(xw[:].bitcast(I32), x_words[0].rearrange("p c r -> p (c r)").bitcast(I32))
+        cand_t = load_list(cand, "cand_t")
+        n1_t = load_list(n1, "n1_t")
+        n2_t = load_list(n2, "n2_t")
+        n3_t = load_list(n3, "n3_t")
+        gs_t = sb.tile([P, PACK], F32, name="gs_t")
+        nc.sync.dma_start(gs_t[:], gs.rearrange("(p t) o -> p (t o)", t=PACK))
+        n4_t = load_list(n4, "n4_t")
+        n5_t = load_list(n5, "n5_t")
+        n6_t = load_list(n6, "n6_t")
+
+        y = [sb.tile([P, 2 * S], F32, name=f"y{t}") for t in range(PACK)]
+        for t in range(PACK):
+            nc.vector.memset(y[t][:, S:], 0.0)
+
+        xq_s = sb.tile([P, S], U8, name="xq_s", align_bytes=64)
+        nc.vector.tensor_copy(xq_s[:], xs[:].indirect(offs_t[:]))
+
+        w_bf = sb.tile([P, PACK, P, PACK], BF16, name="w_bf", align_bytes=64)
+        src = w_raw[:].rearrange("p j (m t) -> p m t j", t=PACK)
+        dst = w_bf[:].rearrange("p t m j -> p m t j")
+        half = P // 2
+        nc.scalar.copy(dst[:, half:], src[:, half:])
+        nc.vector.tensor_copy(dst[:, :half], src[:, :half])
+        w_codes = sb.tile([P, PACK, P], U32, name="w_codes", tag="stationary_codes", align_bytes=64)
+        w_scales = sb.tile([P, PACK, P], U8, name="w_scales", tag="stationary_scales", align_bytes=64)
+
+        def quantize_w(t):
+            nc.vector.quantize_mx(out=w_codes[:, t, :].bitcast(FP8X4), scales=w_scales[:, t, :], in_=w_bf[:, t].rearrange("p m j -> p (m j)"))
+
+        for t in range(PACK):
+            quantize_w(t)
+
+        xq_w = sb.tile([P, S], U32, name="xq_w", align_bytes=64)
+        nc.vector.tensor_copy(xq_w[:], xw[:].indirect(offs_t[:]))
+
+        for t in range(PACK):
+            acc = psum.tile([P, S], F32, name=f"acc_y{t}", tag=f"bank{t}")
+            nc.tensor.matmul_mx(out=acc[:], lhsT=w_codes[:, t, :].bitcast(FP8X4), lhsT_scale=w_scales[:, t, :],
+                                rhs=xq_w[:].bitcast(FP8X4), rhs_scale=xq_s[:], start=True, stop=True)
+            if t == 0:
+                nc.scalar.copy(y[t][:, :S], acc[:])
+            else:
+                nc.vector.tensor_copy(y[t][:, :S], acc[:])
+
+        xc_s = sb.tile([P, C], U8, name="xc_s", tag="stationary_scales", align_bytes=64)
+        for lo in range(0, C, 2 * P):
+            nc.vector.tensor_copy(xc_s[:, lo : lo + 2 * P], xs[:].indirect(entries(cand_t, lo, lo + 2 * P)))
+        xc_w = sb.tile([P, C], U32, name="xc_w", tag="stationary_codes", align_bytes=64)
+        for b in range(BLOCKS):
+            nc.vector.tensor_copy(xc_w[:, b * P : (b + 1) * P], xw[:].indirect(entries(cand_t, b * P, (b + 1) * P)))
+
+        st = [sb.tile([P, 2 * S], F32, name=f"st{t}") for t in range(PACK)]
+        y2 = [sb.tile([P, S], F32, name=f"y2_{t}", tag=f"fetched{t}") for t in range(PACK)]
+        for t in range(PACK):
+            nc.scalar.activation(st[t][:, S:], y[t][:].indirect(n1_t[:]), COPY)
+            nc.scalar.activation(y2[t][:], y[t][:].indirect(n2_t[:]), COPY)
+            nc.vector.tensor_tensor(st[t][:, :S], st[t][:, S:], y2[t][:], ALU.subtract)
+
+        pg = [sb.tile([P, U], F32, name=f"pg{b}") for b in range(BLOCKS)]
+        pieces = ((0, FIRST), (FIRST, S))
+        score = {}
+        for i, (lo, hi) in enumerate(pieces):
+            n = hi - lo
+            z = sb.tile([P, n, PACK], BF16, name=f"z{i}", tag=f"quantised{i}", align_bytes=64)
+            st3_all = sb.tile([P, PACK, n], F32, name=f"st3_{i}", tag="fetched_first" if i == 0 else f"fetched{PACK - 1}")
+            top_all = sb.tile([P, PACK, n], F32, name=f"top_{i}", tag="top_first" if i == 0 else "quantised0", align_bytes=64)
+            for t in range(PACK):
+                st3 = st3_all[:, t, :]
+                top = top_all[:, t, :]
+                window = st[t][:, :S] if i == 0 else st[t][:]
+                nc.scalar.activation(st3, window.indirect(entries(n3_t, lo, hi)), COPY)
+                nc.vector.tensor_tensor(top, st3, st[t][:, lo:hi], ALU.max)
+                nc.vector.tensor_scalar(z[:, :, t], top, gs_t[:, t : t + 1], None, ALU.mult)
+            z_codes = sb.tile([P, n], U32, name=f"z_codes{i}", align_bytes=64)
+            z_scales = sb.tile([P, n], U8, name=f"z_scales{i}", align_bytes=64)
+            cuts = [(0, FIRST)] if i == 0 else [(0, FIRST), (FIRST, n)]
+            for a, e in cuts:
+                nc.vector.quantize_mx(out=z_codes[:, a:e].bitcast(FP8X4), scales=z_scales[:, a:e], in_=z[:, a:e].rearrange("p c t -> p (c t)"))
+            for b in range(BLOCKS):
+                acc = psum.tile([P, n], F32, name=f"acc_s{i}_{b}", tag=f"bank{(4 * (1 - i) + b)}")
+                cols = slice(b * P, (b + 1) * P)
+                for a, e in cuts:
+                    nc.tensor.matmul_mx(out=acc[:, a:e], lhsT=xc_w[:, cols].bitcast(FP8X4), lhsT_scale=xc_s[:, cols],
+                                        rhs=z_codes[:, a:e].bitcast(FP8X4), rhs_scale=z_scales[:, a:e], start=True, stop=True)
+                s = sb.tile([P, n], F32, name=f"s{i}_{b}")
+                nc.vector.tensor_scalar(s[:], acc[:], 0.0625, None, ALU.mult)
+                score[i, b] = s
+
+
+        def put(i, b, slots, factor):
+            lo, hi = pieces[i]
+            nc.scalar.activation(pg[b][:].indirect(entries(slots, lo, hi)), score[i, b][:], COPY, scale=factor)
+
+        def finish(b, cuts):
+            for lo, hi in cuts:
+                far = sb.tile([P, hi - lo], F32, name=f"far{b}_{lo}")
+                res = sb.tile([P, hi - lo], F32, name=f"res{b}_{lo}")
+                nc.scalar.activation(far[:], pg[b][:].indirect(entries(n6_t, lo, hi)), COPY)
+                nc.vector.tensor_tensor(res[:], pg[b][:, lo:hi], far[:], ALU.subtract)
+                nc.sync.dma_start(out[b * P : (b + 1) * P, lo:hi], res[:])
+
+        for slots, factor in ((n4_t, 1.0), (n5_t, 0.5)):
+            for b in range(BLOCKS):
+                put(0, b, slots, factor)
+        halves = ((0, U // 2), (U // 2, U))
+        for pair in ((0, 1), (2, 3)):
+            for slots, factor in ((n4_t, 1.0), (n5_t, 0.5)):
+                for b in pair:
+                    put(1, b, slots, factor)
+            for b in pair:
+                finish(b, halves if b < BLOCKS - 1 else ((0, 256), (256, 384), (384, 512)))

@@ -60,7 +60,7 @@ def tile_picked_candgapmxpagtwo_none_p_kernel(tc, x_words, x_scales, w1, gs, off
         n5_t = load_list(n5, "n5_t")
         n6_t = load_list(n6, "n6_t")
 
-        y = [sb.tile([P, 2 * S], F32, name=f"y{t}") for t in range(PACK)]
+        y = [sb.tile([P, 2 * S], F32, name=f"y{t}", tag=f"projected{t}") for t in range(PACK)]
         for t in range(PACK):
             nc.vector.memset(y[t][:, S:], 0.0)
 
@@ -83,16 +83,19 @@ def tile_picked_candgapmxpagtwo_none_p_kernel(tc, x_words, x_scales, w1, gs, off
             quantize_w(t)
 
         xq_w = sb.tile([P, S], U32, name="xq_w", align_bytes=64)
-        nc.vector.tensor_copy(xq_w[:], xw[:].indirect(offs_t[:]))
+        for lo in range(0, S, P):
+            nc.vector.tensor_copy(xq_w[:, lo : lo + P], xw[:].indirect(entries(offs_t, lo, lo + P)))
 
-        for t in range(PACK):
-            acc = psum.tile([P, S], F32, name=f"acc_y{t}", tag=f"bank{t}")
+        def project(t, lo, hi, bank):
+            acc = psum.tile([P, hi - lo], F32, name=f"acc_y{t}_{lo}", tag=f"bank{bank}")
             nc.tensor.matmul_mx(out=acc[:], lhsT=w_codes[:, t, :].bitcast(FP8X4), lhsT_scale=w_scales[:, t, :],
-                                rhs=xq_w[:].bitcast(FP8X4), rhs_scale=xq_s[:], start=True, stop=True)
-            if t == 0:
-                nc.scalar.copy(y[t][:, :S], acc[:])
-            else:
-                nc.vector.tensor_copy(y[t][:, :S], acc[:])
+                                rhs=xq_w[:, lo:hi].bitcast(FP8X4), rhs_scale=xq_s[:, lo:hi], start=True, stop=True)
+            return acc
+
+        nc.scalar.copy(y[0][:, :P], project(0, 0, P, 0)[:])
+        nc.scalar.copy(y[0][:, P:S], project(0, P, S, PACK)[:])
+        for t in range(1, PACK):
+            nc.vector.tensor_copy(y[t][:, :S], project(t, 0, S, t)[:])
 
         xc_s = sb.tile([P, C], U8, name="xc_s", tag="stationary_scales", align_bytes=64)
         for lo in range(0, C, 2 * P):
@@ -114,34 +117,43 @@ def tile_picked_candgapmxpagtwo_none_p_kernel(tc, x_words, x_scales, w1, gs, off
         for i, (lo, hi) in enumerate(pieces):
             n = hi - lo
             z = sb.tile([P, n, PACK], BF16, name=f"z{i}", tag=f"quantised{i}", align_bytes=64)
-            st3_all = sb.tile([P, PACK, n], F32, name=f"st3_{i}", tag="fetched_first" if i == 0 else f"fetched{PACK - 1}")
+            st3_all = sb.tile([P, PACK, n], F32, name=f"st3_{i}", tag=f"projected{PACK - 2}" if i == 0 else f"fetched{PACK - 1}")
             top_all = sb.tile([P, PACK, n], F32, name=f"top_{i}", tag="top_first" if i == 0 else "quantised0", align_bytes=64)
+            z32 = sb.tile([P, PACK, n], F32, name=f"z32_{i}")
             for t in range(PACK):
                 st3 = st3_all[:, t, :]
                 top = top_all[:, t, :]
                 window = st[t][:, :S] if i == 0 else st[t][:]
                 nc.scalar.activation(st3, window.indirect(entries(n3_t, lo, hi)), COPY)
                 nc.vector.tensor_tensor(top, st3, st[t][:, lo:hi], ALU.max)
-                nc.vector.tensor_scalar(z[:, :, t], top, gs_t[:, t : t + 1], None, ALU.mult)
+                if i == 0:
+                    nc.vector.tensor_scalar(z[:, :, t], top, gs_t[:, t : t + 1], None, ALU.mult)
+                else:
+                    nc.vector.tensor_scalar(z32[:, t, :], top, gs_t[:, t : t + 1], None, ALU.mult)
             z_codes = sb.tile([P, n], U32, name=f"z_codes{i}", align_bytes=64)
             z_scales = sb.tile([P, n], U8, name=f"z_scales{i}", align_bytes=64)
             cuts = [(0, FIRST)] if i == 0 else [(0, FIRST), (FIRST, n)]
+            if i == 1:
+                for a, e in cuts:
+                    nc.vector.tensor_copy(z[:, a:e].rearrange("p (c i) t -> p c t i", i=PACK), z32[:, :, a:e].rearrange("p t (c i) -> p c t i", i=PACK))
             for a, e in cuts:
                 nc.vector.quantize_mx(out=z_codes[:, a:e].bitcast(FP8X4), scales=z_scales[:, a:e], in_=z[:, a:e].rearrange("p c t -> p (c t)"))
-            for b in range(BLOCKS):
-                acc = psum.tile([P, n], F32, name=f"acc_s{i}_{b}", tag=f"bank{(4 * (1 - i) + b)}")
-                cols = slice(b * P, (b + 1) * P)
-                for a, e in cuts:
-                    nc.tensor.matmul_mx(out=acc[:, a:e], lhsT=xc_w[:, cols].bitcast(FP8X4), lhsT_scale=xc_s[:, cols],
-                                        rhs=z_codes[:, a:e].bitcast(FP8X4), rhs_scale=z_scales[:, a:e], start=True, stop=True)
-                s = sb.tile([P, n], F32, name=f"s{i}_{b}")
+            for pair in range(BLOCKS // 2):
+                acc = psum.tile([P, 2, n], F32, name=f"acc_s{i}_{pair}", tag=f"bank{PACK + 1 + pair if i == 0 else pair}")
+                for u in range(2):
+                    cols = slice((2 * pair + u) * P, (2 * pair + u + 1) * P)
+                    for a, e in cuts:
+                        nc.tensor.matmul_mx(out=acc[:, u, a:e], lhsT=xc_w[:, cols].bitcast(FP8X4), lhsT_scale=xc_s[:, cols],
+                                            rhs=z_codes[:, a:e].bitcast(FP8X4), rhs_scale=z_scales[:, a:e], start=True, stop=True)
+                s = sb.tile([P, 2, n], F32, name=f"s{i}_{pair}")
                 nc.vector.tensor_scalar(s[:], acc[:], 0.0625, None, ALU.mult)
-                score[i, b] = s
+                for u in range(2):
+                    score[i, 2 * pair + u] = s[:, u, :]
 
 
         def put(i, b, slots, factor):
             lo, hi = pieces[i]
-            nc.scalar.activation(pg[b][:].indirect(entries(slots, lo, hi)), score[i, b][:], COPY, scale=factor)
+            nc.scalar.activation(pg[b][:].indirect(entries(slots, lo, hi)), score[i, b], COPY, scale=factor)
 
         def finish(b, cuts):
             for lo, hi in cuts:
@@ -154,10 +166,9 @@ def tile_picked_candgapmxpagtwo_none_p_kernel(tc, x_words, x_scales, w1, gs, off
         for slots, factor in ((n4_t, 1.0), (n5_t, 0.5)):
             for b in range(BLOCKS):
                 put(0, b, slots, factor)
-        halves = ((0, U // 2), (U // 2, U))
         for pair in ((0, 1), (2, 3)):
             for slots, factor in ((n4_t, 1.0), (n5_t, 0.5)):
                 for b in pair:
                     put(1, b, slots, factor)
             for b in pair:
-                finish(b, halves if b < BLOCKS - 1 else ((0, 256), (256, 384), (384, 512)))
+                finish(b, ((0, U // 2), (U // 2, U)) if b < BLOCKS - 1 else ((0, U // 2), (U // 2, U - P), (U - P, U)))

@@ -70,17 +70,14 @@ def tile_picked_candgapmxpagtwo_none_p_kernel(tc, x_words, x_scales, w1, gs, off
         w_bf = sb.tile([P, PACK, P, PACK], BF16, name="w_bf", align_bytes=64)
         src = w_raw[:].rearrange("p j (m t) -> p m t j", t=PACK)
         dst = w_bf[:].rearrange("p t m j -> p m t j")
-        half = P // 2
+        half = 72
         nc.scalar.copy(dst[:, half:], src[:, half:])
         nc.vector.tensor_copy(dst[:, :half], src[:, :half])
         w_codes = sb.tile([P, PACK, P], U32, name="w_codes", tag="stationary_codes", align_bytes=64)
-        w_scales = sb.tile([P, PACK, P], U8, name="w_scales", tag="stationary_scales", align_bytes=64)
+        w_scales = sb.tile([P, PACK, P], U8, name="w_scales", align_bytes=64)
 
-        def quantize_w(t):
-            nc.vector.quantize_mx(out=w_codes[:, t, :].bitcast(FP8X4), scales=w_scales[:, t, :], in_=w_bf[:, t].rearrange("p m j -> p (m j)"))
-
-        for t in range(PACK):
-            quantize_w(t)
+        nc.vector.quantize_mx(out=w_codes[:].rearrange("p t m -> p (t m)").bitcast(FP8X4), scales=w_scales[:].rearrange("p t m -> p (t m)"),
+                              in_=w_bf[:].rearrange("p t m j -> p (t m j)"))
 
         xq_w = sb.tile([P, S], U32, name="xq_w", align_bytes=64)
         for lo in range(0, S, P):
@@ -94,12 +91,12 @@ def tile_picked_candgapmxpagtwo_none_p_kernel(tc, x_words, x_scales, w1, gs, off
 
         nc.scalar.copy(y[0][:, :P], project(0, 0, P, 0)[:])
         nc.scalar.copy(y[0][:, P:S], project(0, P, S, PACK)[:])
+        xc_s = sb.tile([P, C], U8, name="xc_s", align_bytes=64)
+        for lo in range(0, C, 2 * P):
+            nc.vector.tensor_copy(xc_s[:, lo : lo + 2 * P], xs[:].indirect(entries(cand_t, lo, lo + 2 * P)))
         for t in range(1, PACK):
             nc.vector.tensor_copy(y[t][:, :S], project(t, 0, S, t)[:])
 
-        xc_s = sb.tile([P, C], U8, name="xc_s", tag="stationary_scales", align_bytes=64)
-        for lo in range(0, C, 2 * P):
-            nc.vector.tensor_copy(xc_s[:, lo : lo + 2 * P], xs[:].indirect(entries(cand_t, lo, lo + 2 * P)))
         xc_w = sb.tile([P, C], U32, name="xc_w", tag="stationary_codes", align_bytes=64)
         for b in range(BLOCKS):
             nc.vector.tensor_copy(xc_w[:, b * P : (b + 1) * P], xw[:].indirect(entries(cand_t, b * P, (b + 1) * P)))
@@ -108,52 +105,50 @@ def tile_picked_candgapmxpagtwo_none_p_kernel(tc, x_words, x_scales, w1, gs, off
         y2 = [sb.tile([P, S], F32, name=f"y2_{t}", tag=f"fetched{t}") for t in range(PACK)]
         for t in range(PACK):
             nc.scalar.activation(st[t][:, S:], y[t][:].indirect(n1_t[:]), COPY)
-            nc.scalar.activation(y2[t][:], y[t][:].indirect(n2_t[:]), COPY)
-            nc.vector.tensor_tensor(st[t][:, :S], st[t][:, S:], y2[t][:], ALU.subtract)
+            for lo, hi in ((0, S),) if t < PACK - 1 else ((0, S - FIRST), (S - FIRST, S)):
+                window = y[t][:] if hi - lo > FIRST else y[t][:, :S]
+                nc.scalar.activation(y2[t][:, lo:hi], window.indirect(entries(n2_t, lo, hi)), COPY)
+                nc.vector.tensor_tensor(st[t][:, lo:hi], st[t][:, S + lo : S + hi], y2[t][:, lo:hi], ALU.subtract)
 
         pg = [sb.tile([P, U], F32, name=f"pg{b}") for b in range(BLOCKS)]
-        pieces = ((0, FIRST), (FIRST, S))
-        score = {}
-        for i, (lo, hi) in enumerate(pieces):
+        z_codes = sb.tile([P, S], U32, name="z_codes", align_bytes=64)
+        z_scales = sb.tile([P, S], U8, name="z_scales", align_bytes=64)
+        rest = sb.tile([P, PACK, S - FIRST], F32, name="st3_rest", tag=f"fetched{PACK - 1}")
+        first = sb.tile([P, PACK, FIRST], F32, name="st3_first", tag=f"projected{PACK - 2}")
+
+        def make_z(lo, hi, st3, z_tag, top_tag):
             n = hi - lo
-            z = sb.tile([P, n, PACK], BF16, name=f"z{i}", tag=f"quantised{i}", align_bytes=64)
-            st3_all = sb.tile([P, PACK, n], F32, name=f"st3_{i}", tag=f"projected{PACK - 2}" if i == 0 else f"fetched{PACK - 1}")
-            top_all = sb.tile([P, PACK, n], F32, name=f"top_{i}", tag="top_first" if i == 0 else "quantised0", align_bytes=64)
-            z32 = sb.tile([P, PACK, n], F32, name=f"z32_{i}")
+            z = sb.tile([P, n, PACK], BF16, name=f"z{lo}", tag=z_tag, align_bytes=64)
+            top = sb.tile([P, PACK, n], F32, name=f"top{lo}", tag=top_tag, align_bytes=64)
             for t in range(PACK):
-                st3 = st3_all[:, t, :]
-                top = top_all[:, t, :]
-                window = st[t][:, :S] if i == 0 else st[t][:]
-                nc.scalar.activation(st3, window.indirect(entries(n3_t, lo, hi)), COPY)
-                nc.vector.tensor_tensor(top, st3, st[t][:, lo:hi], ALU.max)
-                if i == 0:
-                    nc.vector.tensor_scalar(z[:, :, t], top, gs_t[:, t : t + 1], None, ALU.mult)
-                else:
-                    nc.vector.tensor_scalar(z32[:, t, :], top, gs_t[:, t : t + 1], None, ALU.mult)
-            z_codes = sb.tile([P, n], U32, name=f"z_codes{i}", align_bytes=64)
-            z_scales = sb.tile([P, n], U8, name=f"z_scales{i}", align_bytes=64)
-            cuts = [(0, FIRST)] if i == 0 else [(0, FIRST), (FIRST, n)]
-            if i == 1:
-                for a, e in cuts:
-                    nc.vector.tensor_copy(z[:, a:e].rearrange("p (c i) t -> p c t i", i=PACK), z32[:, :, a:e].rearrange("p t (c i) -> p c t i", i=PACK))
-            for a, e in cuts:
-                nc.vector.quantize_mx(out=z_codes[:, a:e].bitcast(FP8X4), scales=z_scales[:, a:e], in_=z[:, a:e].rearrange("p c t -> p (c t)"))
-            for pair in range(BLOCKS // 2):
-                acc = psum.tile([P, 2, n], F32, name=f"acc_s{i}_{pair}", tag=f"bank{PACK + 1 + pair if i == 0 else pair}")
-                for u in range(2):
-                    cols = slice((2 * pair + u) * P, (2 * pair + u + 1) * P)
-                    for a, e in cuts:
-                        nc.tensor.matmul_mx(out=acc[:, u, a:e], lhsT=xc_w[:, cols].bitcast(FP8X4), lhsT_scale=xc_s[:, cols],
-                                            rhs=z_codes[:, a:e].bitcast(FP8X4), rhs_scale=z_scales[:, a:e], start=True, stop=True)
-                s = sb.tile([P, 2, n], F32, name=f"s{i}_{pair}")
-                nc.vector.tensor_scalar(s[:], acc[:], 0.0625, None, ALU.mult)
-                for u in range(2):
-                    score[i, 2 * pair + u] = s[:, u, :]
+                window = st[t][:, :S] if n == FIRST else st[t][:]
+                nc.scalar.activation(st3[:, t, :], window.indirect(entries(n3_t, lo, hi)), COPY)
+                nc.vector.tensor_tensor(top[:, t, :], st3[:, t, :], st[t][:, lo:hi], ALU.max)
+                if lo == 0:
+                    nc.vector.tensor_scalar(z[:, :, t], top[:, t, :], gs_t[:, t : t + 1], None, ALU.mult)
+            if lo > 0:
+                gain = gs_t[:].unsqueeze(1).unsqueeze(3).to_broadcast([P, n // PACK, PACK, PACK])
+                nc.vector.tensor_tensor(z[:].rearrange("p (c i) t -> p c t i", i=PACK), top[:].rearrange("p t (c i) -> p c t i", i=PACK), gain, ALU.mult)
+            nc.vector.quantize_mx(out=z_codes[:, lo:hi].bitcast(FP8X4), scales=z_scales[:, lo:hi], in_=z[:].rearrange("p c t -> p (c t)"))
 
+        def score(blocks, cuts, first_bank):
+            lo, hi = cuts[0], cuts[-1]
+            s = sb.tile([P, len(blocks), hi - lo], F32, name=f"s{lo}_{blocks[0]}")
+            nw = sb.tile([P, len(blocks), hi - lo], F32, name=f"nw{lo}_{blocks[0]}")
+            for u, b in enumerate(blocks):
+                acc = psum.tile([P, hi - lo], F32, name=f"acc_s{lo}_{b}", tag=f"bank{first_bank + b}")
+                cols = slice(b * P, (b + 1) * P)
+                for a, e in zip(cuts, cuts[1:]):
+                    nc.tensor.matmul_mx(out=acc[:, a - lo : e - lo], lhsT=xc_w[:, cols].bitcast(FP8X4), lhsT_scale=xc_s[:, cols],
+                                        rhs=z_codes[:, a:e].bitcast(FP8X4), rhs_scale=z_scales[:, a:e], start=True, stop=True)
+                nc.vector.tensor_scalar(s[:, u, :], acc[:], 0.0625, None, ALU.mult)
+            nc.vector.tensor_scalar(nw[:], s[:], 0.5, None, ALU.mult)
+            return s, nw
 
-        def put(i, b, slots, factor):
-            lo, hi = pieces[i]
-            nc.scalar.activation(pg[b][:].indirect(entries(slots, lo, hi)), score[i, b], COPY, scale=factor)
+        def put(blocks, lo, hi, values):
+            for slots, value in zip((n4_t, n5_t), values):
+                for u, b in enumerate(blocks):
+                    nc.scalar.activation(pg[b][:].indirect(entries(slots, lo, hi)), value[:, u, :], COPY)
 
         def finish(b, cuts):
             for lo, hi in cuts:
@@ -163,12 +158,11 @@ def tile_picked_candgapmxpagtwo_none_p_kernel(tc, x_words, x_scales, w1, gs, off
                 nc.vector.tensor_tensor(res[:], pg[b][:, lo:hi], far[:], ALU.subtract)
                 nc.sync.dma_start(out[b * P : (b + 1) * P, lo:hi], res[:])
 
-        for slots, factor in ((n4_t, 1.0), (n5_t, 0.5)):
-            for b in range(BLOCKS):
-                put(0, b, slots, factor)
+        make_z(0, FIRST, first, "z_first", "top")
+        put(range(BLOCKS), 0, FIRST, score(range(BLOCKS), (0, FIRST), PACK))
+        make_z(FIRST, 2 * FIRST, rest[:, :, :FIRST], "z_second", "top")
+        make_z(2 * FIRST, S, rest[:, :, FIRST:], "z_third", "top")
         for pair in ((0, 1), (2, 3)):
-            for slots, factor in ((n4_t, 1.0), (n5_t, 0.5)):
-                for b in pair:
-                    put(1, b, slots, factor)
+            put(pair, FIRST, S, score(pair, (FIRST, 2 * FIRST, S), 0))
             for b in pair:
                 finish(b, ((0, U // 2), (U // 2, U)) if b < BLOCKS - 1 else ((0, U // 2), (U // 2, U - P), (U - P, U)))

from contextlib import ExitStack

import concourse.mybir as mybir

F32 = mybir.dt.float32
BF16 = mybir.dt.bfloat16
I32 = mybir.dt.int32
U32 = mybir.dt.uint32
U16 = mybir.dt.uint16
U8 = mybir.dt.uint8
FP8X4 = mybir.dt.float8_e4m3fn_x4
COPY = mybir.ActivationFunctionType.Copy
ALU = mybir.AluOpType

P = 128
PACK = 4
T = 2048
S = 256
H = 512
C = 512
U = 512
LANES = 16
BLOCKS = C // P
FIRST = 64
FLOPS = 2 * 512 * H * S + 2 * 512 * C * S


def entries(tile, lo, hi):
    return tile[:, lo // LANES : hi // LANES]


def tile_picked_candgapmxpagtwo_none_p_kernel(tc, x_words, x_scales, w1, gs, offs, n1, n2, n3, cand, n4, n5, n6, out):
    nc = tc.nc
    with ExitStack() as ctx:
        lists = ctx.enter_context(tc.tile_pool(name="lists", bufs=1))
        sb = ctx.enter_context(tc.tile_pool(name="sb", bufs=1))
        psum = ctx.enter_context(tc.psum_pool(name="psum", bufs=1))

        def load_list(src, name):
            tile = lists.tile(list(src.shape), U16, name=name)
            nc.sync.dma_start(tile[:], src)
            return tile

        xs = sb.tile([P, T], U8, name="xs", align_bytes=64)
        nc.vector.memset(xs[:].bitcast(I32), 0)
        w_raw = sb.tile([P, PACK, H], F32, name="w_raw")
        nc.sync.dma_start(w_raw[:], w1.rearrange("(p j) c -> p j c", j=PACK))
        for q in range(4):
            nc.sync.dma_start(xs[32 * q : 32 * q + 4, :].bitcast(I32), x_scales[0, 4 * q : 4 * q + 4, :].bitcast(I32))
        offs_t = load_list(offs, "offs_t")
        xw = sb.tile([P, T], U32, name="xw", align_bytes=64)
        nc.sync.dma_start(xw[:].bitcast(I32), x_words[0].rearrange("p c r -> p (c r)").bitcast(I32))
        cand_t = load_list(cand, "cand_t")
        n1_t = load_list(n1, "n1_t")
        n2_t = load_list(n2, "n2_t")
        n3_t = load_list(n3, "n3_t")
        gs_t = sb.tile([P, PACK], F32, name="gs_t")
        nc.sync.dma_start(gs_t[:], gs.rearrange("(p t) o -> p (t o)", t=PACK))
        n4_t = load_list(n4, "n4_t")
        n5_t = load_list(n5, "n5_t")
        n6_t = load_list(n6, "n6_t")

        y = [sb.tile([P, 2 * S], F32, name=f"y{t}", tag=f"projected{t}") for t in range(PACK)]
        for t in range(PACK):
            nc.vector.memset(y[t][:, S:], 0.0)

        xq_s = sb.tile([P, S], U8, name="xq_s", align_bytes=64)
        nc.vector.tensor_copy(xq_s[:], xs[:].indirect(offs_t[:]))

        w_bf = sb.tile([P, PACK, P, PACK], BF16, name="w_bf", align_bytes=64)
        src = w_raw[:].rearrange("p j (m t) -> p m t j", t=PACK)
        dst = w_bf[:].rearrange("p t m j -> p m t j")
        half = 72
        nc.scalar.copy(dst[:, half:], src[:, half:])
        nc.vector.tensor_copy(dst[:, :half], src[:, :half])
        w_codes = sb.tile([P, PACK, P], U32, name="w_codes", tag="stationary_codes", align_bytes=64)
        w_scales = sb.tile([P, PACK, P], U8, name="w_scales", align_bytes=64)

        nc.vector.quantize_mx(out=w_codes[:].rearrange("p t m -> p (t m)").bitcast(FP8X4), scales=w_scales[:].rearrange("p t m -> p (t m)"),
                              in_=w_bf[:].rearrange("p t m j -> p (t m j)"))

        xq_w = sb.tile([P, S], U32, name="xq_w", align_bytes=64)
        for lo in range(0, S, P):
            nc.vector.tensor_copy(xq_w[:, lo : lo + P], xw[:].indirect(entries(offs_t, lo, lo + P)))

        def project(t, lo, hi, bank):
            acc = psum.tile([P, hi - lo], F32, name=f"acc_y{t}_{lo}", tag=f"bank{bank}")
            nc.tensor.matmul_mx(out=acc[:], lhsT=w_codes[:, t, :].bitcast(FP8X4), lhsT_scale=w_scales[:, t, :],
                                rhs=xq_w[:, lo:hi].bitcast(FP8X4), rhs_scale=xq_s[:, lo:hi], start=True, stop=True)
            return acc

        nc.scalar.copy(y[0][:, :P], project(0, 0, P, 0)[:])
        nc.scalar.copy(y[0][:, P:S], project(0, P, S, PACK)[:])
        xc_s = sb.tile([P, C], U8, name="xc_s", align_bytes=64)
        for lo in range(0, C, 2 * P):
            nc.vector.tensor_copy(xc_s[:, lo : lo + 2 * P], xs[:].indirect(entries(cand_t, lo, lo + 2 * P)))
        for t in range(1, PACK):
            nc.vector.tensor_copy(y[t][:, :S], project(t, 0, S, t)[:])

        xc_w = sb.tile([P, C], U32, name="xc_w", tag="stationary_codes", align_bytes=64)
        for b in range(BLOCKS):
            nc.vector.tensor_copy(xc_w[:, b * P : (b + 1) * P], xw[:].indirect(entries(cand_t, b * P, (b + 1) * P)))

        st = [sb.tile([P, 2 * S], F32, name=f"st{t}") for t in range(PACK)]
        y2 = [sb.tile([P, S], F32, name=f"y2_{t}", tag=f"fetched{t}") for t in range(PACK)]
        for t in range(PACK):
            nc.scalar.activation(st[t][:, S:], y[t][:].indirect(n1_t[:]), COPY)
            for lo, hi in ((0, S),) if t < PACK - 1 else ((0, S - FIRST), (S - FIRST, S)):
                window = y[t][:] if hi - lo > FIRST else y[t][:, :S]
                nc.scalar.activation(y2[t][:, lo:hi], window.indirect(entries(n2_t, lo, hi)), COPY)
                nc.vector.tensor_tensor(st[t][:, lo:hi], st[t][:, S + lo : S + hi], y2[t][:, lo:hi], ALU.subtract)

        pg = [sb.tile([P, U], F32, name=f"pg{b}") for b in range(BLOCKS)]
        z_codes = sb.tile([P, S], U32, name="z_codes", align_bytes=64)
        z_scales = sb.tile([P, S], U8, name="z_scales", align_bytes=64)
        rest = sb.tile([P, PACK, S - FIRST], F32, name="st3_rest", tag=f"fetched{PACK - 1}")
        first = sb.tile([P, PACK, FIRST], F32, name="st3_first", tag=f"projected{PACK - 2}")

        def make_z(lo, hi, st3, z_tag, top_tag):
            n = hi - lo
            z = sb.tile([P, n, PACK], BF16, name=f"z{lo}", tag=z_tag, align_bytes=64)
            top = sb.tile([P, PACK, n], F32, name=f"top{lo}", tag=top_tag, align_bytes=64)
            for t in range(PACK):
                window = st[t][:, :S] if n == FIRST else st[t][:]
                nc.scalar.activation(st3[:, t, :], window.indirect(entries(n3_t, lo, hi)), COPY)
                nc.vector.tensor_tensor(top[:, t, :], st3[:, t, :], st[t][:, lo:hi], ALU.max)
                if lo == 0:
                    nc.vector.tensor_scalar(z[:, :, t], top[:, t, :], gs_t[:, t : t + 1], None, ALU.mult)
            if lo > 0:
                gain = gs_t[:].unsqueeze(1).unsqueeze(3).to_broadcast([P, n // PACK, PACK, PACK])
                nc.vector.tensor_tensor(z[:].rearrange("p (c i) t -> p c t i", i=PACK), top[:].rearrange("p t (c i) -> p c t i", i=PACK), gain, ALU.mult)
            nc.vector.quantize_mx(out=z_codes[:, lo:hi].bitcast(FP8X4), scales=z_scales[:, lo:hi], in_=z[:].rearrange("p c t -> p (c t)"))

        def score(blocks, cuts, first_bank):
            lo, hi = cuts[0], cuts[-1]
            s = sb.tile([P, len(blocks), hi - lo], F32, name=f"s{lo}_{blocks[0]}")
            nw = sb.tile([P, len(blocks), hi - lo], F32, name=f"nw{lo}_{blocks[0]}")
            for u, b in enumerate(blocks):
                acc = psum.tile([P, hi - lo], F32, name=f"acc_s{lo}_{b}", tag=f"bank{first_bank + b}")
                cols = slice(b * P, (b + 1) * P)
                for a, e in zip(cuts, cuts[1:]):
                    nc.tensor.matmul_mx(out=acc[:, a - lo : e - lo], lhsT=xc_w[:, cols].bitcast(FP8X4), lhsT_scale=xc_s[:, cols],
                                        rhs=z_codes[:, a:e].bitcast(FP8X4), rhs_scale=z_scales[:, a:e], start=True, stop=True)
                nc.vector.tensor_scalar(s[:, u, :], acc[:], 0.0625, None, ALU.mult)
            nc.vector.tensor_scalar(nw[:], s[:], 0.5, None, ALU.mult)
            return s, nw

        def put(blocks, lo, hi, values):
            for slots, value in zip((n4_t, n5_t), values):
                for u, b in enumerate(blocks):
                    nc.scalar.activation(pg[b][:].indirect(entries(slots, lo, hi)), value[:, u, :], COPY)

        def finish(b, cuts):
            for lo, hi in cuts:
                far = sb.tile([P, hi - lo], F32, name=f"far{b}_{lo}")
                res = sb.tile([P, hi - lo], F32, name=f"res{b}_{lo}")
                nc.scalar.activation(far[:], pg[b][:].indirect(entries(n6_t, lo, hi)), COPY)
                nc.vector.tensor_tensor(res[:], pg[b][:, lo:hi], far[:], ALU.subtract)
                nc.sync.dma_start(out[b * P : (b + 1) * P, lo:hi], res[:])

        make_z(0, FIRST, first, "z_first", "top")
        put(range(BLOCKS), 0, FIRST, score(range(BLOCKS), (0, FIRST), PACK))
        make_z(FIRST, 2 * FIRST, rest[:, :, :FIRST], "z_second", "top")
        make_z(2 * FIRST, S, rest[:, :, FIRST:], "z_third", "top")
        for pair in ((0, 1), (2, 3)):
            put(pair, FIRST, S, score(pair, (FIRST, 2 * FIRST, S), 0))
            for b in pair:
                finish(b, ((0, U // 2), (U // 2, U)) if b < BLOCKS - 1 else ((0, U // 2), (U // 2, U - P), (U - P, U)))
